import numpy as np
import ml_dtypes


def mxq(x, axis, fmt="e4m3"):
    dtype, down = {"e4m3": (ml_dtypes.float8_e4m3fn, 7), "e5m2": (ml_dtypes.float8_e5m2, 14)}[fmt]
    v = np.moveaxis(np.asarray(x, np.float32).astype(ml_dtypes.bfloat16).astype(np.float64), axis, -1)
    blocks = v.reshape(v.shape[:-1] + (-1, 32))
    amax = np.abs(blocks).max(-1, keepdims=True)
    byte = np.maximum(np.where(amax > 0, np.frexp(amax)[1] - 1 + 127, 0) - down, 1)
    scale = np.exp2(byte - 127.0)
    codes = (blocks / scale).astype(np.float32).astype(dtype).astype(np.float64)
    return np.moveaxis((codes * scale).reshape(v.shape), -1, axis)


WIDE = False


def mx_kscale(k):
    if not WIDE:
        return np.ones(k)
    levels = np.array([30, -30])
    if k % 512:
        return np.exp2(np.random.permutation(np.resize(levels, k // 32))).repeat(32)
    a = np.empty((k // 512, 16))
    for p in range(k // 512):
        a[p, :8] = np.random.permutation(np.resize(levels, 8))
        for g in range(8):
            far = levels[np.abs(levels - a[p, g]) >= 10]
            a[p, g + 8] = far[np.random.randint(len(far))]
    return np.exp2(a.ravel()).repeat(32)


def f64(x):
    return np.asarray(x).astype(np.float64)


def striped(idx):
    return np.tile(np.asarray(idx).reshape(-1, 16).T, (8, 1)).astype(np.uint16)


def unstriped(offs):
    return offs[:16].T.reshape(-1).astype(np.int64)


E2M1 = np.array([0.0, 0.5, 1.0, 1.5, 2.0, 3.0, 4.0, 6.0, -0.0, -0.5, -1.0, -1.5, -2.0, -3.0, -4.0, -6.0])


def pack_weight(w, fmt):
    k, n = w.shape
    w = f64(np.asarray(w, np.float32).astype(ml_dtypes.bfloat16)).reshape(k // 32, 32, n)
    amax = np.abs(w).max(1)
    if fmt in ("e4m3", "e5m2"):
        byte = np.frexp(amax)[1] - 1 + 127 - (7 if fmt == "e4m3" else 14)
    else:
        mant, ex = np.frexp(amax / 6.0)
        byte = np.where(mant > 0.5, ex, ex - 1) + 127
    byte = np.clip(np.where(amax > 0, byte, 1), 1, 254)
    scaled = (w * np.exp2(127.0 - byte)[:, None, :]).reshape(k, n).astype(np.float32)
    by_word = np.ascontiguousarray(scaled.reshape(k // 512, 128, 4, n).transpose(0, 1, 3, 2))
    if fmt in ("e4m3", "e5m2"):
        words = by_word.astype(ml_dtypes.float8_e4m3fn if fmt == "e4m3" else ml_dtypes.float8_e5m2).view(np.uint8)
    else:
        c = by_word.astype(ml_dtypes.float4_e2m1fn).view(np.uint8) & 0xF
        words = (c[..., 0::2] | (c[..., 1::2] << 4)).reshape(k // 512, 128, 2 * n)
    return np.ascontiguousarray(words), np.ascontiguousarray(byte.astype(np.uint8).reshape(k // 512, 16, n))


def unpack_weight(words, scales, fmt):
    g, _, n = scales.shape
    words = np.ascontiguousarray(words).reshape(g, 128, n, -1)
    if fmt in ("e4m3", "e5m2"):
        vals = words.view(ml_dtypes.float8_e4m3fn if fmt == "e4m3" else ml_dtypes.float8_e5m2).astype(np.float64)
    else:
        nib = np.empty((g, 128, n, 4), np.uint8)
        nib[..., 0::2] = words & 0xF
        nib[..., 1::2] = words >> 4
        vals = E2M1[nib]
    vals = vals * np.repeat(np.exp2(scales.astype(np.float64) - 127.0), 8, axis=1)[..., None]
    return vals.transpose(0, 1, 3, 2).reshape(g * 512, n)


def sigmoid(v):
    return 1.0 / (1.0 + np.exp(-v))


K, T, J, R, O, N = 512, 1024, 256, 512, 128, 256


def setup_inputs():
    n = np.random.standard_normal
    idx = np.random.permutation(T)[:J]
    idx2 = np.random.permutation(J)[:O]
    idx3 = np.random.permutation(J)[:O]
    fk = mx_kscale(K)
    fr = mx_kscale(R)
    xtp = pack_weight(n((K, T)) / fk[:, None], "e2m1")
    wp = pack_weight(n((K, R)) * 1 / np.sqrt(K) * fk[:, None], "e4m3")
    w2p = pack_weight(n((K, R)) * 1 / np.sqrt(K) * fk[:, None] * fr, "e5m2")
    wbp = pack_weight(n((R, N)) * 1 / np.sqrt(R) / fr[:, None], "e2m1")
    return {
        "xt_words": xtp[0],
        "xt_scales": xtp[1],
        "w_words": wp[0],
        "w_scales": wp[1],
        "w2_words": w2p[0],
        "w2_scales": w2p[1],
        "sg": (np.random.uniform(0.6, 1.6, (R, 1))).astype(np.float32),
        "bg": (np.random.uniform(-1.0, 1.0, (R, 1))).astype(np.float32),
        "wb_words": wbp[0],
        "wb_scales": wbp[1],
        "offs": striped(idx),
        "offs2": striped(idx2),
        "offs3": striped(idx3),
    }


def reference(xt_words, xt_scales, w_words, w_scales, w2_words, w2_scales, sg, bg, wb_words, wb_scales, offs, offs2, offs3):
    idx = unstriped(offs)
    idx2 = unstriped(offs2)
    idx3 = unstriped(offs3)
    xtu = unpack_weight(xt_words, xt_scales, "e2m1")
    wu = unpack_weight(w_words, w_scales, "e4m3")
    w2u = unpack_weight(w2_words, w2_scales, "e5m2")
    wbu = unpack_weight(wb_words, wb_scales, "e2m1")
    xtidxg = xtu[:, idx]
    a = wu.T @ xtidxg
    b = w2u.T @ xtidxg
    hid = b[:, idx3] * sigmoid(a[:, idx2] * f64(sg) + f64(bg))
    hidq = mxq(hid, 0, "e5m2")
    y = wbu.T @ hidq
    return y

@@ -1,0 +1,174 @@
+from contextlib import ExitStack
+
+import concourse.mybir as mybir
+
+K, T, J, R, O, N = 512, 1024, 256, 512, 128, 256
+FLOPS = 2 * K * R * J * 2 + 2 * R * N * O
+
+F32 = mybir.dt.float32
+BF16 = mybir.dt.bfloat16
+I32 = mybir.dt.int32
+U32 = mybir.dt.uint32
+U16 = mybir.dt.uint16
+U8 = mybir.dt.uint8
+E4M3 = mybir.dt.float8_e4m3fn_x4
+E5M2 = mybir.dt.float8_e5m2_x4
+E2M1 = mybir.dt.float4_e2m1fn_x4
+ACT = mybir.ActivationFunctionType
+
+P = 128
+PACK = 4
+QUADS = 4
+
+
+def load_scale_rows(queue, tile, rows):
+    for q in range(QUADS):
+        queue.dma_start(
+            out=tile[32 * q : 32 * q + 4, :].bitcast(I32),
+            in_=rows[0, 4 * q : 4 * q + 4, :].bitcast(I32),
+        )
+
+
+def deal_columns(copy, dealt, raw, run):
+    copy(
+        out=dealt[:].rearrange("p (t c i) -> p c t i", t=PACK, i=run),
+        in_=raw[:].rearrange("p (c i t) -> p c t i", t=PACK, i=run),
+    )
+
+
+def tile_list_twow_gatefetch_one_plain_kernel(
+    tc, xt_words, xt_scales, w_words, w_scales, w2_words, w2_scales, sg, bg, wb_words, wb_scales, offs, offs2, offs3, out
+):
+    nc = tc.nc
+    with ExitStack() as ctx:
+        sb = ctx.enter_context(tc.tile_pool(name="sb", bufs=1))
+        psum = ctx.enter_context(tc.psum_pool(name="psum", bufs=1))
+
+        tok_list = sb.tile([P, J // 16], U16)
+        gate_list = sb.tile([P, O // 16], U16)
+        val_list = sb.tile([P, O // 16], U16)
+        xt_w = sb.tile([P, T], U16, align_bytes=64)
+        xt_s = sb.tile([P, T], U8, align_bytes=64)
+        w_raw = sb.tile([P, R], U32, align_bytes=64)
+        w_s_raw = sb.tile([P, R], U8, align_bytes=64)
+        w2_raw = sb.tile([P, R], U32, align_bytes=64)
+        w2_s_raw = sb.tile([P, R], U8, align_bytes=64)
+        wb_w = sb.tile([P, 2 * N], U8, align_bytes=64)
+        wb_s = sb.tile([P, N], U8, align_bytes=64)
+        slope = sb.tile([P, PACK], F32)
+        offset = sb.tile([P, PACK], F32)
+
+        nc.vector.memset(xt_s[:].bitcast(I32), 0)
+        nc.vector.memset(w2_s_raw[:].bitcast(I32), 0)
+        nc.vector.memset(w_s_raw[:].bitcast(I32), 0)
+        nc.vector.memset(wb_s[:].bitcast(I32), 0)
+        warm_in = sb.tile([P, 1], F32)
+        warm_out = sb.tile([P, 1], F32)
+        nc.vector.memset(warm_in[:], 0.0)
+        nc.scalar.activation(out=warm_out[:], in_=warm_in[:], func=ACT.Sigmoid)
+
+        nc.sync.dma_start(tok_list[:], offs)
+        nc.sync.dma_start(out=xt_w[:].bitcast(I32), in_=xt_words[0].bitcast(I32))
+        load_scale_rows(nc.sync, xt_s, xt_scales)
+        nc.sync.dma_start(out=w2_raw[:].bitcast(I32), in_=w2_words[0].rearrange("p n t -> p (n t)").bitcast(I32))
+        nc.sync.dma_start(out=w_raw[:].bitcast(I32), in_=w_words[0].rearrange("p n t -> p (n t)").bitcast(I32))
+        load_scale_rows(nc.sync, w2_s_raw, w2_scales)
+        load_scale_rows(nc.sync, w_s_raw, w_scales)
+        nc.sync.dma_start(val_list[:], offs3)
+        nc.sync.dma_start(gate_list[:], offs2)
+        nc.sync.dma_start(out=slope[:], in_=sg.rearrange("(p t) o -> p (t o)", t=PACK))
+        nc.sync.dma_start(out=offset[:], in_=bg.rearrange("(p t) o -> p (t o)", t=PACK))
+        nc.sync.dma_start(out=wb_w[:].bitcast(I32), in_=wb_words[0].bitcast(I32))
+        load_scale_rows(nc.sync, wb_s, wb_scales)
+
+        x_w = sb.tile([P, J], U16, align_bytes=64)
+        x_s = sb.tile([P, J], U8, align_bytes=64)
+        nc.vector.tensor_copy(x_w[:], xt_w[:].indirect(tok_list[:]))
+        nc.vector.tensor_copy(x_s[:], xt_s[:].indirect(tok_list[:]))
+
+        w_w = sb.tile([P, R], U32, align_bytes=64)
+        w_s = sb.tile([P, R], U8, align_bytes=64)
+        w2_w = sb.tile([P, R], U32, align_bytes=64)
+        w2_s = sb.tile([P, R], U8, align_bytes=64)
+        deal_columns(nc.scalar.copy, w2_w, w2_raw, 4)
+        deal_columns(nc.vector.tensor_copy, w2_s, w2_s_raw, 16)
+        deal_columns(nc.scalar.copy, w_w, w_raw, 4)
+        deal_columns(nc.vector.tensor_copy, w_s, w_s_raw, 16)
+
+        def first_stage(words, scales, fmt, t, bank):
+            acc = psum.tile([P, J], F32, name="acc%d" % bank, tag="bank%d" % bank)
+            cols = slice(P * t, P * (t + 1))
+            nc.tensor.matmul_mx(
+                out=acc[:],
+                lhsT=words[:, cols].bitcast(fmt),
+                lhsT_scale=scales[:, cols],
+                rhs=x_w[:].bitcast(E2M1),
+                rhs_scale=x_s[:],
+                start=True,
+                stop=True,
+            )
+            return acc
+
+        gate = sb.tile([P, PACK, O], F32)
+        picked = sb.tile([P, PACK, O], F32)
+        b_rows = []
+        for t in range(PACK):
+            acc = first_stage(w2_w, w2_s, E5M2, t, t)
+            rows = sb.tile([P, J], F32, name="b_rows%d" % t)
+            if t % 2 == 0:
+                nc.vector.tensor_copy(out=rows[:], in_=acc[:])
+            else:
+                nc.scalar.copy(out=rows[:], in_=acc[:])
+            b_rows.append(rows)
+
+        def pick(t):
+            if t == 0:
+                nc.scalar.activation(out=picked[:, t, :], in_=b_rows[t][:].indirect(val_list[:]), func=ACT.Copy)
+            else:
+                nc.vector.tensor_copy(picked[:, t, :], b_rows[t][:].indirect(val_list[:]))
+
+        pick(0)
+        pick(1)
+        for t in range(PACK):
+            acc = first_stage(w_w, w_s, E4M3, t, PACK + t)
+            a_rows = sb.tile([P, J], F32, name="a_rows%d" % t)
+            nc.vector.tensor_copy(out=a_rows[:], in_=acc[:])
+            nc.scalar.activation(
+                out=gate[:, t, :],
+                in_=a_rows[:].indirect(gate_list[:]),
+                func=ACT.Sigmoid,
+                bias=offset[:, t : t + 1],
+                scale=slope[:, t : t + 1],
+            )
+        pick(2)
+        pick(3)
+
+        hid = sb.tile([P, O, PACK], BF16, align_bytes=64)
+        nc.vector.tensor_tensor(
+            out=hid[:].rearrange("p (c i) t -> p c t i", i=4),
+            in0=picked[:].rearrange("p t (c i) -> p c t i", i=4),
+            in1=gate[:].rearrange("p t (c i) -> p c t i", i=4),
+            op=mybir.AluOpType.mult,
+        )
+        hid_w = sb.tile([P, O], U32, align_bytes=64)
+        hid_s = sb.tile([P, O], U8, align_bytes=64)
+        nc.vector.quantize_mx(out=hid_w[:].bitcast(E5M2), scales=hid_s[:], in_=hid[:].rearrange("p o t -> p (o t)"))
+
+        for h in range(N // P):
+            acc = psum.tile([P, O], F32, name="y%d" % h, tag="bank%d" % h)
+            nc.tensor.matmul_mx(
+                out=acc[:],
+                lhsT=wb_w[:, 2 * P * h : 2 * P * (h + 1)].bitcast(E2M1),
+                lhsT_scale=wb_s[:, P * h : P * (h + 1)],
+                rhs=hid_w[:].bitcast(E5M2),
+                rhs_scale=hid_s[:],
+                start=True,
+                stop=True,
+            )
+            y = sb.tile([P, O], F32, name="y_rows%d" % h)
+            if h == 0:
+                nc.vector.tensor_copy(out=y[:], in_=acc[:])
+                nc.sync.dma_start(out=out[P * h : P * (h + 1), :], in_=y[:])
+            else:
+                nc.scalar.copy(out=y[:], in_=acc[:])
+                nc.scalar.dma_start(out=out[P * h : P * (h + 1), :], in_=y[:])

@@ -21,18 +21,18 @@ PACK = 4
 QUADS = 4
 
 
-def load_scale_rows(queue, tile, rows):
-    for q in range(QUADS):
+def load_scale_rows(queue, tile, rows, quads=range(QUADS)):
+    for q in quads:
         queue.dma_start(
             out=tile[32 * q : 32 * q + 4, :].bitcast(I32),
             in_=rows[0, 4 * q : 4 * q + 4, :].bitcast(I32),
         )
 
 
-def deal_columns(copy, dealt, raw, run):
+def deal_columns(copy, dealt, raw, run, slots=slice(0, PACK)):
     copy(
-        out=dealt[:].rearrange("p (t c i) -> p c t i", t=PACK, i=run),
-        in_=raw[:].rearrange("p (c i t) -> p c t i", t=PACK, i=run),
+        out=dealt[:].rearrange("p (t c i) -> p c t i", t=PACK, i=run)[:, :, slots, :],
+        in_=raw[:].rearrange("p (c i t) -> p c t i", t=PACK, i=run)[:, :, slots, :],
     )
 
 
@@ -50,7 +50,7 @@ def tile_list_twow_gatefetch_one_plain_kernel(
         xt_w = sb.tile([P, T], U16, align_bytes=64)
         xt_s = sb.tile([P, T], U8, align_bytes=64)
         w_raw = sb.tile([P, R], U32, align_bytes=64)
-        w_s_raw = sb.tile([P, R], U8, align_bytes=64)
+        w_s_raw = sb.tile([P, R], U8, tag="w_s_raw", align_bytes=64)
         w2_raw = sb.tile([P, R], U32, align_bytes=64)
         w2_s_raw = sb.tile([P, R], U8, align_bytes=64)
         wb_w = sb.tile([P, 2 * N], U8, align_bytes=64)
@@ -71,8 +71,9 @@ def tile_list_twow_gatefetch_one_plain_kernel(
         nc.sync.dma_start(out=xt_w[:].bitcast(I32), in_=xt_words[0].bitcast(I32))
         load_scale_rows(nc.sync, xt_s, xt_scales)
         nc.sync.dma_start(out=w2_raw[:].bitcast(I32), in_=w2_words[0].rearrange("p n t -> p (n t)").bitcast(I32))
+        load_scale_rows(nc.sync, w2_s_raw, w2_scales, range(0, 1))
         nc.sync.dma_start(out=w_raw[:].bitcast(I32), in_=w_words[0].rearrange("p n t -> p (n t)").bitcast(I32))
-        load_scale_rows(nc.sync, w2_s_raw, w2_scales)
+        load_scale_rows(nc.sync, w2_s_raw, w2_scales, range(1, QUADS))
         load_scale_rows(nc.sync, w_s_raw, w_scales)
         nc.sync.dma_start(val_list[:], offs3)
         nc.sync.dma_start(gate_list[:], offs2)
@@ -91,9 +92,11 @@ def tile_list_twow_gatefetch_one_plain_kernel(
         w2_w = sb.tile([P, R], U32, align_bytes=64)
         w2_s = sb.tile([P, R], U8, align_bytes=64)
         deal_columns(nc.scalar.copy, w2_w, w2_raw, 4)
-        deal_columns(nc.vector.tensor_copy, w2_s, w2_s_raw, 16)
+        deal_columns(nc.vector.tensor_copy, w2_s, w2_s_raw, 16, slice(0, 1))
+        deal_columns(nc.vector.tensor_copy, w2_s, w2_s_raw, 16, slice(1, PACK))
         deal_columns(nc.scalar.copy, w_w, w_raw, 4)
-        deal_columns(nc.vector.tensor_copy, w_s, w_s_raw, 16)
+        deal_columns(nc.vector.tensor_copy, w_s, w_s_raw, 16, slice(0, 1))
+        deal_columns(nc.vector.tensor_copy, w_s, w_s_raw, 16, slice(1, PACK))
 
         def first_stage(words, scales, fmt, t, bank):
             acc = psum.tile([P, J], F32, name="acc%d" % bank, tag="bank%d" % bank)
@@ -111,24 +114,20 @@ def tile_list_twow_gatefetch_one_plain_kernel(
 
         gate = sb.tile([P, PACK, O], F32)
         picked = sb.tile([P, PACK, O], F32)
+        b_odd = sb.tile([P, 2, J], F32, tag="w_s_raw", align_bytes=64)
         b_rows = []
         for t in range(PACK):
             acc = first_stage(w2_w, w2_s, E5M2, t, t)
-            rows = sb.tile([P, J], F32, name="b_rows%d" % t)
             if t % 2 == 0:
-                nc.vector.tensor_copy(out=rows[:], in_=acc[:])
-            else:
+                rows = sb.tile([P, J], F32, name="b_rows%d" % t)
                 nc.scalar.copy(out=rows[:], in_=acc[:])
-            b_rows.append(rows)
-
-        def pick(t):
-            if t == 0:
-                nc.scalar.activation(out=picked[:, t, :], in_=b_rows[t][:].indirect(val_list[:]), func=ACT.Copy)
+                b_rows.append(rows[:])
             else:
-                nc.vector.tensor_copy(picked[:, t, :], b_rows[t][:].indirect(val_list[:]))
+                nc.vector.tensor_copy(out=b_odd[:, t // 2, :], in_=acc[:])
+                b_rows.append(b_odd[:, t // 2, :])
 
-        pick(0)
-        pick(1)
+        for t in (0, 2):
+            nc.scalar.activation(out=picked[:, t, :], in_=b_rows[t].indirect(val_list[:]), func=ACT.Copy)
         for t in range(PACK):
             acc = first_stage(w_w, w_s, E4M3, t, PACK + t)
             a_rows = sb.tile([P, J], F32, name="a_rows%d" % t)
@@ -140,8 +139,8 @@ def tile_list_twow_gatefetch_one_plain_kernel(
                 bias=offset[:, t : t + 1],
                 scale=slope[:, t : t + 1],
             )
-        pick(2)
-        pick(3)
+        for t in (1, 3):
+            nc.vector.tensor_copy(picked[:, t, :], b_rows[t].indirect(val_list[:]))
 
         hid = sb.tile([P, O, PACK], BF16, align_bytes=64)
         nc.vector.tensor_tensor(

from contextlib import ExitStack

import concourse.mybir as mybir

K, T, J, R, O, N = 512, 1024, 256, 512, 128, 256
FLOPS = 2 * K * R * J * 2 + 2 * R * N * O

F32 = mybir.dt.float32
BF16 = mybir.dt.bfloat16
I32 = mybir.dt.int32
U32 = mybir.dt.uint32
U16 = mybir.dt.uint16
U8 = mybir.dt.uint8
E4M3 = mybir.dt.float8_e4m3fn_x4
E5M2 = mybir.dt.float8_e5m2_x4
E2M1 = mybir.dt.float4_e2m1fn_x4
ACT = mybir.ActivationFunctionType

P = 128
PACK = 4
QUADS = 4


def load_scale_rows(queue, tile, rows, quads=range(QUADS)):
    for q in quads:
        queue.dma_start(
            out=tile[32 * q : 32 * q + 4, :].bitcast(I32),
            in_=rows[0, 4 * q : 4 * q + 4, :].bitcast(I32),
        )


def deal_columns(copy, dealt, raw, run, slots=slice(0, PACK)):
    copy(
        out=dealt[:].rearrange("p (t c i) -> p c t i", t=PACK, i=run)[:, :, slots, :],
        in_=raw[:].rearrange("p (c i t) -> p c t i", t=PACK, i=run)[:, :, slots, :],
    )


def tile_list_twow_gatefetch_one_plain_kernel(
    tc, xt_words, xt_scales, w_words, w_scales, w2_words, w2_scales, sg, bg, wb_words, wb_scales, offs, offs2, offs3, out
):
    nc = tc.nc
    with ExitStack() as ctx:
        sb = ctx.enter_context(tc.tile_pool(name="sb", bufs=1))
        psum = ctx.enter_context(tc.psum_pool(name="psum", bufs=1))

        tok_list = sb.tile([P, J // 16], U16)
        gate_list = sb.tile([P, O // 16], U16)
        val_list = sb.tile([P, O // 16], U16)
        xt_w = sb.tile([P, T], U16, align_bytes=64)
        xt_s = sb.tile([P, T], U8, align_bytes=64)
        w_raw = sb.tile([P, R], U32, align_bytes=64)
        w_s_raw = sb.tile([P, R], U8, tag="w_s_raw", align_bytes=64)
        w2_raw = sb.tile([P, R], U32, align_bytes=64)
        w2_s_raw = sb.tile([P, R], U8, align_bytes=64)
        wb_w = sb.tile([P, 2 * N], U8, align_bytes=64)
        wb_s = sb.tile([P, N], U8, align_bytes=64)
        slope = sb.tile([P, PACK], F32)
        offset = sb.tile([P, PACK], F32)

        nc.vector.memset(xt_s[:].bitcast(I32), 0)
        nc.vector.memset(w2_s_raw[:].bitcast(I32), 0)
        nc.vector.memset(w_s_raw[:].bitcast(I32), 0)
        nc.vector.memset(wb_s[:].bitcast(I32), 0)
        warm_in = sb.tile([P, 1], F32)
        warm_out = sb.tile([P, 1], F32)
        nc.vector.memset(warm_in[:], 0.0)
        nc.scalar.activation(out=warm_out[:], in_=warm_in[:], func=ACT.Sigmoid)

        nc.sync.dma_start(tok_list[:], offs)
        nc.sync.dma_start(out=xt_w[:].bitcast(I32), in_=xt_words[0].bitcast(I32))
        load_scale_rows(nc.sync, xt_s, xt_scales)
        nc.sync.dma_start(out=w2_raw[:].bitcast(I32), in_=w2_words[0].rearrange("p n t -> p (n t)").bitcast(I32))
        load_scale_rows(nc.sync, w2_s_raw, w2_scales, range(0, 1))
        nc.sync.dma_start(out=w_raw[:].bitcast(I32), in_=w_words[0].rearrange("p n t -> p (n t)").bitcast(I32))
        load_scale_rows(nc.sync, w2_s_raw, w2_scales, range(1, QUADS))
        load_scale_rows(nc.sync, w_s_raw, w_scales)
        nc.sync.dma_start(val_list[:], offs3)
        nc.sync.dma_start(gate_list[:], offs2)
        nc.sync.dma_start(out=slope[:], in_=sg.rearrange("(p t) o -> p (t o)", t=PACK))
        nc.sync.dma_start(out=offset[:], in_=bg.rearrange("(p t) o -> p (t o)", t=PACK))
        nc.sync.dma_start(out=wb_w[:].bitcast(I32), in_=wb_words[0].bitcast(I32))
        load_scale_rows(nc.sync, wb_s, wb_scales)

        x_w = sb.tile([P, J], U16, align_bytes=64)
        x_s = sb.tile([P, J], U8, align_bytes=64)
        nc.vector.tensor_copy(x_w[:], xt_w[:].indirect(tok_list[:]))
        nc.vector.tensor_copy(x_s[:], xt_s[:].indirect(tok_list[:]))

        w_w = sb.tile([P, R], U32, align_bytes=64)
        w_s = sb.tile([P, R], U8, align_bytes=64)
        w2_w = sb.tile([P, R], U32, align_bytes=64)
        w2_s = sb.tile([P, R], U8, align_bytes=64)
        deal_columns(nc.scalar.copy, w2_w, w2_raw, 4)
        deal_columns(nc.vector.tensor_copy, w2_s, w2_s_raw, 16, slice(0, 1))
        deal_columns(nc.vector.tensor_copy, w2_s, w2_s_raw, 16, slice(1, PACK))
        deal_columns(nc.scalar.copy, w_w, w_raw, 4)
        deal_columns(nc.vector.tensor_copy, w_s, w_s_raw, 16, slice(0, 1))
        deal_columns(nc.vector.tensor_copy, w_s, w_s_raw, 16, slice(1, PACK))

        def first_stage(words, scales, fmt, t, bank):
            acc = psum.tile([P, J], F32, name="acc%d" % bank, tag="bank%d" % bank)
            cols = slice(P * t, P * (t + 1))
            nc.tensor.matmul_mx(
                out=acc[:],
                lhsT=words[:, cols].bitcast(fmt),
                lhsT_scale=scales[:, cols],
                rhs=x_w[:].bitcast(E2M1),
                rhs_scale=x_s[:],
                start=True,
                stop=True,
            )
            return acc

        gate = sb.tile([P, PACK, O], F32)
        picked = sb.tile([P, PACK, O], F32)
        b_odd = sb.tile([P, 2, J], F32, tag="w_s_raw", align_bytes=64)
        b_rows = []
        for t in range(PACK):
            acc = first_stage(w2_w, w2_s, E5M2, t, t)
            if t % 2 == 0:
                rows = sb.tile([P, J], F32, name="b_rows%d" % t)
                nc.scalar.copy(out=rows[:], in_=acc[:])
                b_rows.append(rows[:])
            else:
                nc.vector.tensor_copy(out=b_odd[:, t // 2, :], in_=acc[:])
                b_rows.append(b_odd[:, t // 2, :])

        for t in (0, 2):
            nc.scalar.activation(out=picked[:, t, :], in_=b_rows[t].indirect(val_list[:]), func=ACT.Copy)
        for t in range(PACK):
            acc = first_stage(w_w, w_s, E4M3, t, PACK + t)
            a_rows = sb.tile([P, J], F32, name="a_rows%d" % t)
            nc.vector.tensor_copy(out=a_rows[:], in_=acc[:])
            nc.scalar.activation(
                out=gate[:, t, :],
                in_=a_rows[:].indirect(gate_list[:]),
                func=ACT.Sigmoid,
                bias=offset[:, t : t + 1],
                scale=slope[:, t : t + 1],
            )
        for t in (1, 3):
            nc.vector.tensor_copy(picked[:, t, :], b_rows[t].indirect(val_list[:]))

        hid = sb.tile([P, O, PACK], BF16, align_bytes=64)
        nc.vector.tensor_tensor(
            out=hid[:].rearrange("p (c i) t -> p c t i", i=4),
            in0=picked[:].rearrange("p t (c i) -> p c t i", i=4),
            in1=gate[:].rearrange("p t (c i) -> p c t i", i=4),
            op=mybir.AluOpType.mult,
        )
        hid_w = sb.tile([P, O], U32, align_bytes=64)
        hid_s = sb.tile([P, O], U8, align_bytes=64)
        nc.vector.quantize_mx(out=hid_w[:].bitcast(E5M2), scales=hid_s[:], in_=hid[:].rearrange("p o t -> p (o t)"))

        for h in range(N // P):
            acc = psum.tile([P, O], F32, name="y%d" % h, tag="bank%d" % h)
            nc.tensor.matmul_mx(
                out=acc[:],
                lhsT=wb_w[:, 2 * P * h : 2 * P * (h + 1)].bitcast(E2M1),
                lhsT_scale=wb_s[:, P * h : P * (h + 1)],
                rhs=hid_w[:].bitcast(E5M2),
                rhs_scale=hid_s[:],
                start=True,
                stop=True,
            )
            y = sb.tile([P, O], F32, name="y_rows%d" % h)
            if h == 0:
                nc.vector.tensor_copy(out=y[:], in_=acc[:])
                nc.sync.dma_start(out=out[P * h : P * (h + 1), :], in_=y[:])
            else:
                nc.scalar.copy(out=y[:], in_=acc[:])
                nc.scalar.dma_start(out=out[P * h : P * (h + 1), :], in_=y[:])
